import numpy as np
import ml_dtypes


def mxq(x, axis, fmt="e4m3"):
    dtype, down = {"e4m3": (ml_dtypes.float8_e4m3fn, 7), "e5m2": (ml_dtypes.float8_e5m2, 14)}[fmt]
    v = np.moveaxis(np.asarray(x, np.float32).astype(ml_dtypes.bfloat16).astype(np.float64), axis, -1)
    blocks = v.reshape(v.shape[:-1] + (-1, 32))
    amax = np.abs(blocks).max(-1, keepdims=True)
    byte = np.maximum(np.where(amax > 0, np.frexp(amax)[1] - 1 + 127, 0) - down, 1)
    scale = np.exp2(byte - 127.0)
    codes = (blocks / scale).astype(np.float32).astype(dtype).astype(np.float64)
    return np.moveaxis((codes * scale).reshape(v.shape), -1, axis)


WIDE = False


def mx_kscale(k):
    if not WIDE:
        return np.ones(k)
    levels = np.array([10, -10, 5, -5, 0])
    if k % 512:
        return np.exp2(np.random.permutation(np.resize(levels, k // 32))).repeat(32)
    a = np.empty((k // 512, 16))
    for p in range(k // 512):
        a[p, :8] = np.random.permutation(np.resize(levels, 8))
        for g in range(8):
            far = levels[np.abs(levels - a[p, g]) >= 10]
            a[p, g + 8] = far[np.random.randint(len(far))]
    return np.exp2(a.ravel()).repeat(32)


def f64(x):
    return np.asarray(x).astype(np.float64)


def striped(idx):
    return np.tile(idx.reshape(-1, 16).T, (8, 1)).astype(np.uint16)


def unstriped(offs):
    return offs[:16].T.reshape(-1).astype(np.int64)


E2M1 = np.array([0.0, 0.5, 1.0, 1.5, 2.0, 3.0, 4.0, 6.0, -0.0, -0.5, -1.0, -1.5, -2.0, -3.0, -4.0, -6.0])


def pack_weight(w, fmt):
    k, n = w.shape
    w = f64(np.asarray(w, np.float32).astype(ml_dtypes.bfloat16)).reshape(k // 32, 32, n)
    amax = np.abs(w).max(1)
    if fmt == "e4m3":
        byte = np.frexp(amax)[1] - 1 + 127 - 7
    else:
        mant, ex = np.frexp(amax / 6.0)
        byte = np.where(mant > 0.5, ex, ex - 1) + 127
    byte = np.clip(np.where(amax > 0, byte, 1), 1, 254)
    scaled = (w * np.exp2(127.0 - byte)[:, None, :]).reshape(k, n).astype(np.float32)
    by_word = np.ascontiguousarray(scaled.reshape(k // 512, 128, 4, n).transpose(0, 1, 3, 2))
    if fmt == "e4m3":
        words = by_word.astype(ml_dtypes.float8_e4m3fn).view(np.uint8)
    else:
        c = by_word.astype(ml_dtypes.float4_e2m1fn).view(np.uint8) & 0xF
        words = (c[..., 0::2] | (c[..., 1::2] << 4)).reshape(k // 512, 128, 2 * n)
    return np.ascontiguousarray(words), np.ascontiguousarray(byte.astype(np.uint8).reshape(k // 512, 16, n))


def unpack_weight(words, scales, fmt):
    g, _, n = scales.shape
    words = np.ascontiguousarray(words).reshape(g, 128, n, -1)
    if fmt == "e4m3":
        vals = words.view(ml_dtypes.float8_e4m3fn).astype(np.float64)
    else:
        nib = np.empty((g, 128, n, 4), np.uint8)
        nib[..., 0::2] = words & 0xF
        nib[..., 1::2] = words >> 4
        vals = E2M1[nib]
    vals = vals * np.repeat(np.exp2(scales.astype(np.float64) - 127.0), 8, axis=1)[..., None]
    return vals.transpose(0, 1, 3, 2).reshape(g * 512, n)


def gelu(v):
    return 0.5 * v * (1.0 + np.tanh(np.sqrt(2.0 / np.pi) * (v + 0.044715 * v**3)))


K, K2, H, N, T, T3, S, P = 1024, 512, 1024, 512, 4096, 2048, 1024, 512

def setup_inputs():
    n = np.random.standard_normal
    s = mx_kscale(K)[:, None]
    s2 = mx_kscale(K2)[:, None]
    u = mx_kscale(H)[:, None]
    d = {}
    d["tab_words"], d["tab_scales"] = pack_weight(n((K, T)) * s, "e4m3")
    d["offs"] = striped(np.random.permutation(T)[:S])
    d["tab2_words"], d["tab2_scales"] = pack_weight(n((K2, T3)) * s2, "e4m3")
    d["offs2"] = striped(np.random.permutation(T3)[:P])
    d["pos1"] = striped(np.random.permutation(S)[:P])
    d["w1"] = (3.0 * np.exp(0.5 * n((1, H))) * n((K, H)) / K ** 0.5 / s).astype(np.float32)
    w2 = 4.0 * np.exp(0.5 * n((1, H))) * n((K2, H)) / K2 ** 0.5 / s2
    d["w2_words"], d["w2_scales"] = pack_weight(w2, "e2m1")
    d["wgs"] = np.exp(0.3 * n((128, P)) + 0.7).astype(np.float32)
    d["gain"] = (np.exp(0.3 * n(H)) * u[:, 0]).astype(np.float32)
    d["w4"] = (n((H, N)) / H ** 0.5 / u).astype(np.float32)
    d["base"] = n(N).astype(np.float32)
    return d

def reference(tab_words, tab_scales, offs, tab2_words, tab2_scales, offs2, pos1, w1, w2_words, w2_scales, wgs, gain, w4, base):
    v = unpack_weight(tab_words, tab_scales, "e4m3")[:, unstriped(offs)]
    v2 = unpack_weight(tab2_words, tab2_scales, "e4m3")[:, unstriped(offs2)]
    a = mxq(f64(w1), 0, "e4m3").T @ v
    y2 = unpack_weight(w2_words, w2_scales, "e2m1").T @ v2
    b = np.log(1.0 + np.abs(y2))
    placed = np.zeros((H, S))
    placed[:, unstriped(pos1)] = np.tile(f64(wgs), (H // 128, 1)) * b
    z = f64(gain)[:, None] * np.sqrt(1.0 + np.abs(a + placed))
    y = mxq(f64(w4), 0, "e4m3").T @ mxq(z, 0, "e4m3")
    return y - f64(base)[:, None]

@@ -1,0 +1,290 @@
+from contextlib import ExitStack
+
+import concourse.mybir as mybir
+
+F32 = mybir.dt.float32
+BF16 = mybir.dt.bfloat16
+I32 = mybir.dt.int32
+U32 = mybir.dt.uint32
+U16 = mybir.dt.uint16
+U8 = mybir.dt.uint8
+FP8X4 = mybir.dt.float8_e4m3fn_x4
+FP4X4 = mybir.dt.float4_e2m1fn_x4
+ACT = mybir.ActivationFunctionType
+ALU = mybir.AluOpType
+
+K, K2, H, N, T, T3, S, PB = 1024, 512, 1024, 512, 4096, 2048, 1024, 512
+FLOPS = 2 * (K * H * S + K2 * H * PB + H * N * S)
+
+P = 128
+PACK = 4
+KP = P * PACK
+HALF = 512
+PAGES = 3
+
+
+def tile_list_burrow_activity_features_kernel(
+    tc, tab_words, tab_scales, offs, tab2_words, tab2_scales, offs2, pos1, w1, w2_words, w2_scales, wgs, gain, w4, base, out
+):
+    nc = tc.nc
+    with ExitStack() as ctx:
+        keep = ctx.enter_context(tc.tile_pool(name="keep", bufs=1))
+        ring = ctx.enter_context(tc.tile_pool(name="ring", bufs=2))
+        rawp = ctx.enter_context(tc.tile_pool(name="rawp", bufs=4))
+        psum = ctx.enter_context(tc.psum_pool(name="psum", bufs=8))
+
+        offs_t = keep.tile([P, S // 16], U16, name="offs_t")
+        offs2_t = keep.tile([P, PB // 16], U16, name="offs2_t")
+        pos_t = keep.tile([P, PB // 16], U16, name="pos_t")
+        t2w = keep.tile([P, T3], I32, name="t2w")
+        t2s = keep.tile([P, T3], U8, name="t2s")
+        w2w = keep.tile([P, 2 * H], U8, name="w2w")
+        w2s = keep.tile([P, H], U8, name="w2s")
+        tw = [keep.tile([P, T], I32, name="tw%d" % a, align_bytes=64) for a in range(2)]
+        ts = keep.tile([P, T], U8, name="ts", align_bytes=64)
+        wg = keep.tile([P, PACK * PB], F32, name="wg")
+        gain_t = keep.tile([P, 2, PACK], F32, name="gain_t")
+        base_t = keep.tile([P, N // P], F32, name="base_t")
+        nbase = keep.tile([P, N // P], F32, name="nbase")
+        pages = [keep.tile([P, S], F32, name="page%d" % i) for i in range(PAGES)]
+        warm = keep.tile([P, 3], F32, name="warm")
+
+        nc.gpsimd.memset(t2s[:].bitcast(I32), 0)
+        nc.vector.memset(w2s[:].bitcast(I32), 0)
+        nc.gpsimd.memset(warm[:, 0:1], 1.0)
+        nc.gpsimd.memset(ts[:].bitcast(I32), 0)
+
+        nc.sync.dma_start(offs2_t[:], offs2)
+        nc.sync.dma_start(w2w[:].bitcast(I32), w2_words[0].bitcast(I32))
+        nc.sync.dma_start(t2w[:], tab2_words[0].rearrange("p n t -> p (n t)").bitcast(I32))
+        for q in range(4):
+            nc.scalar.dma_start(t2s[32 * q : 32 * q + 4, :].bitcast(I32), tab2_scales[0, 4 * q : 4 * q + 4, :].bitcast(I32))
+        nc.scalar.activation(warm[:, 1:2], warm[:, 0:1], ACT.Ln)
+        for q in range(4):
+            nc.scalar.dma_start(ts[32 * q : 32 * q + 8, :].bitcast(I32), tab_scales[:, 4 * q : 4 * q + 4, :].bitcast(I32))
+        for q in range(4):
+            nc.sync.dma_start(w2s[32 * q : 32 * q + 4, :].bitcast(I32), w2_scales[0, 4 * q : 4 * q + 4, :].bitcast(I32))
+        nc.sync.dma_start(pos_t[:], pos1)
+        wgs_rows = wgs.rearrange("(q t) m -> q (t m)", t=PACK)
+        for q in range(4):
+            nc.sync.dma_start(wg[32 * q : 32 * q + 32, :], wgs_rows)
+        for page in pages:
+            nc.gpsimd.memset(page[:], 0.0)
+        nc.sync.dma_start(offs_t[:], offs)
+
+        def load_w1(g, a):
+            raw = rawp.tile([P, PACK, KP], F32, name="raw")
+            nc.sync.dma_start(raw[:], w1[a * KP : (a + 1) * KP, g * KP : (g + 1) * KP].rearrange("(p j) c -> p j c", j=PACK))
+            return raw
+
+        def load_w4(g):
+            raw = rawp.tile([P, PACK, N], F32, name="raw")
+            nc.sync.dma_start(raw[:], w4[g * KP : (g + 1) * KP, :].rearrange("(p j) c -> p j c", j=PACK))
+            return raw
+
+        w1raw = {}
+        for a in range(2):
+            w1raw[0, a] = load_w1(0, a)
+        for a in range(2):
+            nc.sync.dma_start(tw[a][:], tab_words[a].rearrange("p n t -> p (n t)").bitcast(I32))
+        for a in range(2):
+            w1raw[1, a] = load_w1(1, a)
+        nc.sync.dma_start(gain_t[:], gain.rearrange("(g p t) -> p g t", g=2, t=PACK))
+        with nc.allow_non_contiguous_dma(reason="one bias value a partition"):
+            nc.sync.dma_start(base_t[:], base.rearrange("(c p) -> p c", p=P))
+
+        w2d = [keep.tile([P, 2 * KP], U8, name="w2d%d" % g, align_bytes=64) for g in range(2)]
+        w2sd = [keep.tile([P, KP], U8, name="w2sd%d" % g, align_bytes=64) for g in range(2)]
+        v2w = keep.tile([P, PB], U32, name="v2w", align_bytes=64)
+        v2s = keep.tile([P, PB], U8, name="v2s", align_bytes=64)
+        def deal_words(g):
+            nc.vector.tensor_copy(
+                w2d[g][:].rearrange("p (t m b) -> p t m b", t=PACK, b=2),
+                w2w[:, g * 2 * KP : (g + 1) * 2 * KP].rearrange("p (m t b) -> p t m b", t=PACK, b=2),
+            )
+
+        def deal_scales(g):
+            nc.vector.tensor_copy(
+                w2sd[g][:].rearrange("p (t m) -> p t m", t=PACK),
+                w2s[:, g * KP : (g + 1) * KP].rearrange("p (m t) -> p t m", t=PACK),
+            )
+
+        nc.vector.tensor_copy(v2w[:], t2w[:].bitcast(U32).indirect(offs2_t[:]))
+        nc.vector.tensor_copy(v2s[:], t2s[:].indirect(offs2_t[:]))
+        for g in range(2):
+            deal_words(g)
+            deal_scales(g)
+
+        b = []
+        for i in range(8):
+            g, t = divmod(i, PACK)
+            acc = psum.tile([P, PB], F32, name="acc")
+            nc.tensor.matmul_mx(
+                out=acc[:],
+                lhsT=w2d[g][:, 2 * P * t : 2 * P * (t + 1)].bitcast(FP4X4),
+                lhsT_scale=w2sd[g][:, P * t : P * (t + 1)],
+                rhs=v2w[:].bitcast(FP8X4),
+                rhs_scale=v2s[:],
+                start=True,
+                stop=True,
+            )
+            bi = keep.tile([P, PB], F32, name="b%d" % i, align_bytes=64)
+            nc.scalar.activation(bi[:], acc[:], ACT.Abs)
+            nc.scalar.activation(bi[:], bi[:], ACT.Ln, bias=1.0)
+            b.append(bi)
+
+        def page_of(i):
+            return pages[i if i < PAGES else 2 - min(i, 6) % 2]
+
+        nc.scalar.activation(warm[:, 2:3], b[7][:, 0:1], ACT.Sqrt, bias=1.0)
+
+        def scatter(i):
+            t = i % PACK
+            nc.vector.tensor_tensor(page_of(i)[:].indirect(pos_t[:]), b[i][:], wg[:, t * PB : (t + 1) * PB], ALU.mult)
+
+        def quantise(name, grouped, width=KP, tag=None):
+            codes = keep.tile([P, width], U32, name=name + "_codes", tag=tag or name + "_codes", align_bytes=64)
+            scales = keep.tile([P, width], U8, name=name + "_scales", align_bytes=64)
+            nc.vector.quantize_mx(out=codes[:].bitcast(FP8X4), scales=scales[:], in_=grouped[:])
+            return codes, scales
+
+        def cast_w1(g, a):
+            grouped = ring.tile([P, PACK * KP], BF16, name="wbf", align_bytes=64, bufs=4)
+            nc.scalar.copy(
+                grouped[:].rearrange("p (u v m j) -> p m u j v", u=2, v=2, j=PACK),
+                w1raw[g, a][:].rearrange("p j (m u v) -> p m u j v", u=2, v=2),
+            )
+            return grouped
+
+        def cast_w4(raw):
+            grouped = ring.tile([P, PACK * N], BF16, name="wbf", align_bytes=64, bufs=4)
+            nc.scalar.copy(
+                grouped[:].rearrange("p (c i j) -> p c j i", i=2, j=PACK),
+                raw[:].rearrange("p j (c i) -> p c j i", i=2),
+            )
+            return grouped
+
+        for i in range(PAGES):
+            scatter(i)
+
+        casts = [cast_w1(0, a) for a in range(2)]
+        w4raw = [load_w4(g) for g in range(2)]
+
+        vw = {}
+        vs = {}
+        for h in range(2):
+            cols = offs_t[:, h * HALF // 16 : (h + 1) * HALF // 16]
+            for a in range(2):
+                vw[a, h] = keep.tile([P, HALF], U32, name="vw%d%d" % (a, h), align_bytes=64)
+            vs[h] = keep.tile([P, HALF], U8, name="vs%d" % h, align_bytes=64)
+            nc.vector.tensor_copy(vw[0, h][:], tw[0][:].bitcast(U32).indirect(cols))
+            nc.vector.tensor_copy(vs[h][:], ts[:].indirect(cols))
+            nc.vector.tensor_copy(vw[1, h][:], tw[1][:].bitcast(U32).indirect(cols))
+
+        w1q = {}
+        w1q[0, 0] = quantise("w1q00", casts[0], tag="ts")
+        w1q[0, 1] = quantise("w1q01", casts[1], tag="tw0")
+        lev = {(g, h): keep.tile([P, PACK, HALF], F32, name="lev%d%d" % (g, h), align_bytes=64) for g in range(2) for h in range(2)}
+
+        def level(i, h):
+            g, t = divmod(i, PACK)
+            acc = psum.tile([P, HALF], F32, name="acc")
+            for a in range(2):
+                codes, scales = w1q[g, a]
+                nc.tensor.matmul_mx(
+                    out=acc[:],
+                    lhsT=codes[:, P * t : P * (t + 1)].bitcast(FP8X4),
+                    lhsT_scale=scales[:, P * t : P * (t + 1)],
+                    rhs=vw[a, h][:].bitcast(FP8X4),
+                    rhs_scale=vs[h][4 * a : P, :],
+                    start=(a == 0),
+                    stop=(a == 1),
+                )
+            dst = lev[g, h][:, t, :]
+            nc.vector.tensor_tensor(dst, acc[:], page_of(i)[:, h * HALF : (h + 1) * HALF], ALU.add)
+            nc.scalar.activation(dst, dst, ACT.Abs)
+            nc.scalar.activation(dst, dst, ACT.Sqrt, bias=1.0)
+
+        def z_on_vector(g, j0, width, tag):
+            h, c0 = divmod(j0, HALF)
+            grouped = keep.tile([P, PACK * width], BF16, name="zbf%d_%d" % (g, j0), tag=tag, align_bytes=64)
+            nc.vector.tensor_tensor(
+                grouped[:].rearrange("p (c i t) -> p c t i", i=2, t=PACK),
+                lev[g, h][:, :, c0 : c0 + width].rearrange("p t (c i) -> p c t i", i=2),
+                gain_t[:, g, :].unsqueeze(1).unsqueeze(3).broadcast_to([P, width // 2, PACK, 2]),
+                ALU.mult,
+            )
+            return grouped
+
+        def z_on_scalar(g, h):
+            planes = keep.tile([P, PACK, HALF], BF16, name="zpl", tag="b7", align_bytes=64)
+            for t in range(PACK):
+                nc.scalar.activation(planes[:, t, :], lev[g, h][:, t, :], ACT.Copy, scale=gain_t[:, g, t : t + 1])
+            grouped = keep.tile([P, PACK * HALF], BF16, name="zbf", align_bytes=64)
+            nc.scalar.copy(
+                grouped[:].rearrange("p (c i t) -> p c t i", i=4, t=PACK),
+                planes[:].rearrange("p t (c i) -> p c t i", i=4),
+            )
+            return grouped
+
+        def features(j0, width, z0, z1, engines):
+            for pair in range(2):
+                res = rawp.tile([P, 2, width], F32, name="res", bufs=6)
+                for e in range(2):
+                    c = 2 * pair + e
+                    acc = psum.tile([P, width], F32, name="acc")
+                    for g, (codes, scales, c0) in enumerate((z0, z1)):
+                        nc.tensor.matmul_mx(
+                            out=acc[:],
+                            lhsT=w4q[g][0][:, P * c : P * (c + 1)].bitcast(FP8X4),
+                            lhsT_scale=w4q[g][1][:, P * c : P * (c + 1)],
+                            rhs=codes[:, c0 : c0 + width].bitcast(FP8X4),
+                            rhs_scale=scales[:, c0 : c0 + width],
+                            start=(g == 0),
+                            stop=(g == 1),
+                        )
+                    if engines[pair] == "vector":
+                        nc.vector.tensor_scalar(res[:, e, :], acc[:], base_t[:, c : c + 1], None, ALU.subtract)
+                    else:
+                        nc.scalar.activation(res[:, e, :], acc[:], ACT.Identity, bias=nbase[:, c : c + 1])
+                rows = out[2 * P * pair : 2 * P * (pair + 1), j0 : j0 + width].rearrange("(e p) j -> p e j", p=P)
+                nc.sync.dma_start(rows, res[:])
+
+        nc.gpsimd.tensor_scalar(nbase[:], base_t[:], -1.0, 0.0, ALU.mult, ALU.add)
+
+        def levels(i):
+            for h in range(2):
+                level(i, h)
+
+        casts = [cast_w1(1, a) for a in range(2)]
+        levels(0)
+        levels(1)
+        scatter(3)
+        for a in range(2):
+            w1q[1, a] = quantise("w1q1%d" % a, casts[a], tag="b%d" % (3 + a))
+        casts = [cast_w4(w4raw[g]) for g in range(2)]
+        levels(2)
+        scatter(4)
+        levels(3)
+        scatter(5)
+        levels(4)
+        scatter(6)
+        levels(5)
+        z00 = z_on_vector(0, 0, HALF, "b6")
+        levels(6)
+        scatter(7)
+        levels(7)
+        Q = HALF // 2
+        q00 = quantise("zq00", z00)
+        w4q = [quantise("w4q%d" % g, casts[g], tag="b%d" % (5 - 5 * g)) for g in range(2)]
+        z10 = z_on_vector(1, 0, HALF, "tw1")
+        q10 = quantise("zq10", z10)
+        z01 = z_on_scalar(0, 1)
+        features(0, HALF, q00 + (0,), q10 + (0,), ("scalar", "scalar"))
+        z11a = z_on_vector(1, HALF, Q, "b1")
+        q01 = quantise("zq01", z01)
+        z11b = z_on_vector(1, HALF + Q, Q, "b2")
+        q11a = quantise("zq11a", z11a, Q)
+        q11b = quantise("zq11b", z11b, Q)
+        features(HALF, Q, q01 + (0,), q11a + (0,), ("scalar", "vector"))
+        features(HALF + Q, Q, q01 + (Q,), q11b + (0,), ("scalar", "vector"))

@@ -29,7 +29,6 @@ def tile_list_burrow_activity_features_kernel(
     nc = tc.nc
     with ExitStack() as ctx:
         keep = ctx.enter_context(tc.tile_pool(name="keep", bufs=1))
-        ring = ctx.enter_context(tc.tile_pool(name="ring", bufs=2))
         rawp = ctx.enter_context(tc.tile_pool(name="rawp", bufs=4))
         psum = ctx.enter_context(tc.psum_pool(name="psum", bufs=8))
 
@@ -51,8 +50,9 @@ def tile_list_burrow_activity_features_kernel(
 
         nc.gpsimd.memset(t2s[:].bitcast(I32), 0)
         nc.vector.memset(w2s[:].bitcast(I32), 0)
-        nc.gpsimd.memset(warm[:, 0:1], 1.0)
-        nc.gpsimd.memset(ts[:].bitcast(I32), 0)
+        nc.gpsimd.memset(ts[:, : T // 2].bitcast(I32), 0)
+        nc.vector.memset(ts[:, T // 2 :].bitcast(I32), 0)
+        nc.vector.memset(warm[:, 0:1], 1.0)
 
         nc.sync.dma_start(offs2_t[:], offs2)
         nc.sync.dma_start(w2w[:].bitcast(I32), w2_words[0].bitcast(I32))
@@ -61,16 +61,16 @@ def tile_list_burrow_activity_features_kernel(
             nc.scalar.dma_start(t2s[32 * q : 32 * q + 4, :].bitcast(I32), tab2_scales[0, 4 * q : 4 * q + 4, :].bitcast(I32))
         nc.scalar.activation(warm[:, 1:2], warm[:, 0:1], ACT.Ln)
         for q in range(4):
-            nc.scalar.dma_start(ts[32 * q : 32 * q + 8, :].bitcast(I32), tab_scales[:, 4 * q : 4 * q + 4, :].bitcast(I32))
-        for q in range(4):
             nc.sync.dma_start(w2s[32 * q : 32 * q + 4, :].bitcast(I32), w2_scales[0, 4 * q : 4 * q + 4, :].bitcast(I32))
+        for q in range(4):
+            nc.sync.dma_start(ts[32 * q : 32 * q + 8, :].bitcast(I32), tab_scales[:, 4 * q : 4 * q + 4, :].bitcast(I32))
+        nc.sync.dma_start(offs_t[:], offs)
         nc.sync.dma_start(pos_t[:], pos1)
         wgs_rows = wgs.rearrange("(q t) m -> q (t m)", t=PACK)
         for q in range(4):
             nc.sync.dma_start(wg[32 * q : 32 * q + 32, :], wgs_rows)
         for page in pages:
             nc.gpsimd.memset(page[:], 0.0)
-        nc.sync.dma_start(offs_t[:], offs)
 
         def load_w1(g, a):
             raw = rawp.tile([P, PACK, KP], F32, name="raw")
@@ -145,56 +145,61 @@ def tile_list_burrow_activity_features_kernel(
         def quantise(name, grouped, width=KP, tag=None):
             codes = keep.tile([P, width], U32, name=name + "_codes", tag=tag or name + "_codes", align_bytes=64)
             scales = keep.tile([P, width], U8, name=name + "_scales", align_bytes=64)
-            nc.vector.quantize_mx(out=codes[:].bitcast(FP8X4), scales=scales[:], in_=grouped[:])
+            nc.vector.quantize_mx(out=codes[:].bitcast(FP8X4), scales=scales[:], in_=grouped)
             return codes, scales
 
-        def cast_w1(g, a):
-            grouped = ring.tile([P, PACK * KP], BF16, name="wbf", align_bytes=64, bufs=4)
-            nc.scalar.copy(
-                grouped[:].rearrange("p (u v m j) -> p m u j v", u=2, v=2, j=PACK),
-                w1raw[g, a][:].rearrange("p j (m u v) -> p m u j v", u=2, v=2),
-            )
-            return grouped
+        def cast_w1(g):
+            grouped = keep.tile([P, 2, PACK * KP], BF16, name="wbf%d" % g, align_bytes=64)
+            for a in range(2):
+                nc.scalar.copy(
+                    grouped[:, a, :].rearrange("p (u v m j) -> p m u j v", u=2, v=2, j=PACK),
+                    w1raw[g, a][:].rearrange("p j (m u v) -> p m u j v", u=2, v=2),
+                )
+            return grouped[:].rearrange("p a c -> p (a c)")
 
-        def cast_w4(raw):
-            grouped = ring.tile([P, PACK * N], BF16, name="wbf", align_bytes=64, bufs=4)
-            nc.scalar.copy(
-                grouped[:].rearrange("p (c i j) -> p c j i", i=2, j=PACK),
-                raw[:].rearrange("p j (c i) -> p c j i", i=2),
-            )
-            return grouped
+        def cast_w4():
+            grouped = keep.tile([P, 2, PACK * N], BF16, name="w4bf", tag="tw1", align_bytes=64)
+            for g in range(2):
+                nc.scalar.copy(
+                    grouped[:, g, :].rearrange("p (c i j) -> p c j i", i=2, j=PACK),
+                    w4raw[g][:].rearrange("p j (c i) -> p c j i", i=2),
+                )
+            return grouped[:].rearrange("p g c -> p (g c)")
 
         for i in range(PAGES):
             scatter(i)
 
-        casts = [cast_w1(0, a) for a in range(2)]
+        cast0 = cast_w1(0)
         w4raw = [load_w4(g) for g in range(2)]
 
         vw = {}
         vs = {}
-        for h in range(2):
-            cols = offs_t[:, h * HALF // 16 : (h + 1) * HALF // 16]
-            for a in range(2):
-                vw[a, h] = keep.tile([P, HALF], U32, name="vw%d%d" % (a, h), align_bytes=64)
-            vs[h] = keep.tile([P, HALF], U8, name="vs%d" % h, align_bytes=64)
-            nc.vector.tensor_copy(vw[0, h][:], tw[0][:].bitcast(U32).indirect(cols))
-            nc.vector.tensor_copy(vs[h][:], ts[:].indirect(cols))
-            nc.vector.tensor_copy(vw[1, h][:], tw[1][:].bitcast(U32).indirect(cols))
-
         w1q = {}
-        w1q[0, 0] = quantise("w1q00", casts[0], tag="ts")
-        w1q[0, 1] = quantise("w1q01", casts[1], tag="tw0")
+
+        def gather_words(a, h, tag):
+            vw[a, h] = keep.tile([P, HALF], U32, name="vw%d%d" % (a, h), tag=tag, align_bytes=64)
+            nc.vector.tensor_copy(vw[a, h][:], tw[a][:].bitcast(U32).indirect(offs_t[:, h * HALF // 16 : (h + 1) * HALF // 16]))
+
+        for h in range(2):
+            vs[h] = keep.tile([P, HALF], U8, name="vs%d" % h, align_bytes=64)
+            nc.vector.tensor_copy(vs[h][:], ts[:].indirect(offs_t[:, h * HALF // 16 : (h + 1) * HALF // 16]))
+        gather_words(0, 0, "vw00")
+        gather_words(0, 1, "vw01")
+        gather_words(1, 0, "vw10")
+        w1q[0] = quantise("w1q0", cast0, 2 * KP, tag="tw0")
+        gather_words(1, 1, "wbf0")
         lev = {(g, h): keep.tile([P, PACK, HALF], F32, name="lev%d%d" % (g, h), align_bytes=64) for g in range(2) for h in range(2)}
 
         def level(i, h):
             g, t = divmod(i, PACK)
             acc = psum.tile([P, HALF], F32, name="acc")
             for a in range(2):
-                codes, scales = w1q[g, a]
+                codes, scales = w1q[g]
+                cols = slice(a * KP + P * t, a * KP + P * (t + 1))
                 nc.tensor.matmul_mx(
                     out=acc[:],
-                    lhsT=codes[:, P * t : P * (t + 1)].bitcast(FP8X4),
-                    lhsT_scale=scales[:, P * t : P * (t + 1)],
+                    lhsT=codes[:, cols].bitcast(FP8X4),
+                    lhsT_scale=scales[:, cols],
                     rhs=vw[a, h][:].bitcast(FP8X4),
                     rhs_scale=vs[h][4 * a : P, :],
                     start=(a == 0),
@@ -214,7 +219,7 @@ def tile_list_burrow_activity_features_kernel(
                 gain_t[:, g, :].unsqueeze(1).unsqueeze(3).broadcast_to([P, width // 2, PACK, 2]),
                 ALU.mult,
             )
-            return grouped
+            return grouped[:]
 
         def z_on_scalar(g, h):
             planes = keep.tile([P, PACK, HALF], BF16, name="zpl", tag="b7", align_bytes=64)
@@ -225,7 +230,7 @@ def tile_list_burrow_activity_features_kernel(
                 grouped[:].rearrange("p (c i t) -> p c t i", i=4, t=PACK),
                 planes[:].rearrange("p t (c i) -> p c t i", i=4),
             )
-            return grouped
+            return grouped[:]
 
         def features(j0, width, z0, z1, engines):
             for pair in range(2):
@@ -236,8 +241,8 @@ def tile_list_burrow_activity_features_kernel(
                     for g, (codes, scales, c0) in enumerate((z0, z1)):
                         nc.tensor.matmul_mx(
                             out=acc[:],
-                            lhsT=w4q[g][0][:, P * c : P * (c + 1)].bitcast(FP8X4),
-                            lhsT_scale=w4q[g][1][:, P * c : P * (c + 1)],
+                            lhsT=w4q[0][:, g * N + P * c : g * N + P * (c + 1)].bitcast(FP8X4),
+                            lhsT_scale=w4q[1][:, g * N + P * c : g * N + P * (c + 1)],
                             rhs=codes[:, c0 : c0 + width].bitcast(FP8X4),
                             rhs_scale=scales[:, c0 : c0 + width],
                             start=(g == 0),
@@ -256,13 +261,12 @@ def tile_list_burrow_activity_features_kernel(
             for h in range(2):
                 level(i, h)
 
-        casts = [cast_w1(1, a) for a in range(2)]
+        cast1 = cast_w1(1)
         levels(0)
         levels(1)
         scatter(3)
-        for a in range(2):
-            w1q[1, a] = quantise("w1q1%d" % a, casts[a], tag="b%d" % (3 + a))
-        casts = [cast_w4(w4raw[g]) for g in range(2)]
+        w1q[1] = quantise("w1q1", cast1, 2 * KP, tag="b3")
+        cast4 = cast_w4()
         levels(2)
         scatter(4)
         levels(3)
@@ -276,8 +280,8 @@ def tile_list_burrow_activity_features_kernel(
         levels(7)
         Q = HALF // 2
         q00 = quantise("zq00", z00)
-        w4q = [quantise("w4q%d" % g, casts[g], tag="b%d" % (5 - 5 * g)) for g in range(2)]
-        z10 = z_on_vector(1, 0, HALF, "tw1")
+        w4q = quantise("w4q", cast4, 2 * N, tag="b5")
+        z10 = z_on_vector(1, 0, HALF, "wbf1")
         q10 = quantise("zq10", z10)
         z01 = z_on_scalar(0, 1)
         features(0, HALF, q00 + (0,), q10 + (0,), ("scalar", "scalar"))

@@ -136,8 +136,6 @@ def tile_list_burrow_activity_features_kernel(
         def page_of(i):
             return pages[i if i < PAGES else 2 - min(i, 6) % 2]
 
-        nc.scalar.activation(warm[:, 2:3], b[7][:, 0:1], ACT.Sqrt, bias=1.0)
-
         def scatter(i):
             t = i % PACK
             nc.vector.tensor_tensor(page_of(i)[:].indirect(pos_t[:]), b[i][:], wg[:, t * PB : (t + 1) * PB], ALU.mult)
@@ -152,24 +150,23 @@ def tile_list_burrow_activity_features_kernel(
             grouped = keep.tile([P, 2, PACK * KP], BF16, name="wbf%d" % g, align_bytes=64)
             for a in range(2):
                 nc.scalar.copy(
-                    grouped[:, a, :].rearrange("p (u v m j) -> p m u j v", u=2, v=2, j=PACK),
-                    w1raw[g, a][:].rearrange("p j (m u v) -> p m u j v", u=2, v=2),
+                    grouped[:, a, :].rearrange("p (t m j) -> p m t j", t=PACK, j=PACK),
+                    w1raw[g, a][:].rearrange("p j (m t) -> p m t j", t=PACK),
                 )
             return grouped[:].rearrange("p a c -> p (a c)")
 
         def cast_w4():
             grouped = keep.tile([P, 2, PACK * N], BF16, name="w4bf", tag="tw1", align_bytes=64)
             for g in range(2):
-                nc.scalar.copy(
-                    grouped[:, g, :].rearrange("p (c i j) -> p c j i", i=2, j=PACK),
-                    w4raw[g][:].rearrange("p j (c i) -> p c j i", i=2),
-                )
+                copy = nc.vector.tensor_copy if g == 1 else nc.scalar.copy
+                copy(grouped[:, g, :].rearrange("p (c j) -> p c j", j=PACK), w4raw[g][:].rearrange("p j c -> p c j"))
             return grouped[:].rearrange("p g c -> p (g c)")
 
         for i in range(PAGES):
             scatter(i)
 
         cast0 = cast_w1(0)
+        nc.scalar.activation(warm[:, 2:3], b[7][:, 0:1], ACT.Sqrt, bias=1.0)
         w4raw = [load_w4(g) for g in range(2)]
 
         vw = {}
@@ -188,7 +185,7 @@ def tile_list_burrow_activity_features_kernel(
         gather_words(1, 0, "vw10")
         w1q[0] = quantise("w1q0", cast0, 2 * KP, tag="tw0")
         gather_words(1, 1, "wbf0")
-        lev = {(g, h): keep.tile([P, PACK, HALF], F32, name="lev%d%d" % (g, h), align_bytes=64) for g in range(2) for h in range(2)}
+        planes = {(g, h): keep.tile([P, PACK, HALF], BF16, name="zpl%d%d" % (g, h)) for g in range(2) for h in range(2)}
 
         def level(i, h):
             g, t = divmod(i, PACK)
@@ -205,36 +202,31 @@ def tile_list_burrow_activity_features_kernel(
                     start=(a == 0),
                     stop=(a == 1),
                 )
-            dst = lev[g, h][:, t, :]
+            if i == 6:
+                lev = keep.tile([P, HALF], F32, name="lev6%d" % h, tag="zpl0%d" % h)
+            else:
+                lev = rawp.tile([P, HALF], F32, name="lev", bufs=8)
+            dst = lev[:]
             nc.vector.tensor_tensor(dst, acc[:], page_of(i)[:, h * HALF : (h + 1) * HALF], ALU.add)
             nc.scalar.activation(dst, dst, ACT.Abs)
             nc.scalar.activation(dst, dst, ACT.Sqrt, bias=1.0)
+            if i == 7:
+                nc.vector.tensor_scalar(planes[g, h][:, t, :], dst, gain_t[:, g, t : t + 1], None, ALU.mult)
+            else:
+                nc.scalar.activation(planes[g, h][:, t, :], dst, ACT.Copy, scale=gain_t[:, g, t : t + 1])
 
         def z_on_vector(g, j0, width, tag):
             h, c0 = divmod(j0, HALF)
             grouped = keep.tile([P, PACK * width], BF16, name="zbf%d_%d" % (g, j0), tag=tag, align_bytes=64)
-            nc.vector.tensor_tensor(
-                grouped[:].rearrange("p (c i t) -> p c t i", i=2, t=PACK),
-                lev[g, h][:, :, c0 : c0 + width].rearrange("p t (c i) -> p c t i", i=2),
-                gain_t[:, g, :].unsqueeze(1).unsqueeze(3).broadcast_to([P, width // 2, PACK, 2]),
-                ALU.mult,
-            )
-            return grouped[:]
-
-        def z_on_scalar(g, h):
-            planes = keep.tile([P, PACK, HALF], BF16, name="zpl", tag="b7", align_bytes=64)
-            for t in range(PACK):
-                nc.scalar.activation(planes[:, t, :], lev[g, h][:, t, :], ACT.Copy, scale=gain_t[:, g, t : t + 1])
-            grouped = keep.tile([P, PACK * HALF], BF16, name="zbf", align_bytes=64)
-            nc.scalar.copy(
-                grouped[:].rearrange("p (c i t) -> p c t i", i=4, t=PACK),
-                planes[:].rearrange("p t (c i) -> p c t i", i=4),
+            nc.vector.tensor_copy(
+                grouped[:].rearrange("p (c t) -> p c t", t=PACK),
+                planes[g, h][:, :, c0 : c0 + width].rearrange("p t c -> p c t"),
             )
             return grouped[:]
 
         def features(j0, width, z0, z1, engines):
             for pair in range(2):
-                res = rawp.tile([P, 2, width], F32, name="res", bufs=6)
+                res = rawp.tile([P, 2, width], F32, name="res", bufs=8)
                 for e in range(2):
                     c = 2 * pair + e
                     acc = psum.tile([P, width], F32, name="acc")
@@ -274,21 +266,16 @@ def tile_list_burrow_activity_features_kernel(
         levels(4)
         scatter(6)
         levels(5)
-        z00 = z_on_vector(0, 0, HALF, "b6")
+        z00 = z_on_vector(0, 0, HALF, "b0")
+        z01 = z_on_vector(0, HALF, HALF, "b4")
+        q00 = quantise("zq00", z00)
         levels(6)
         scatter(7)
         levels(7)
         Q = HALF // 2
-        q00 = quantise("zq00", z00)
-        w4q = quantise("w4q", cast4, 2 * N, tag="b5")
-        z10 = z_on_vector(1, 0, HALF, "wbf1")
-        q10 = quantise("zq10", z10)
-        z01 = z_on_scalar(0, 1)
-        features(0, HALF, q00 + (0,), q10 + (0,), ("scalar", "scalar"))
-        z11a = z_on_vector(1, HALF, Q, "b1")
-        q01 = quantise("zq01", z01)
-        z11b = z_on_vector(1, HALF + Q, Q, "b2")
-        q11a = quantise("zq11a", z11a, Q)
-        q11b = quantise("zq11b", z11b, Q)
-        features(HALF, Q, q01 + (0,), q11a + (0,), ("scalar", "vector"))
-        features(HALF + Q, Q, q01 + (Q,), q11b + (0,), ("scalar", "vector"))
+        w4q = quantise("w4q", cast4, 2 * N, tag="b7")
+        q01 = quantise("zq01", z01, tag="b6")
+        for piece in range(4):
+            h, c0 = divmod(piece * Q, HALF)
+            z1 = quantise("zq1%d" % piece, z_on_vector(1, piece * Q, Q, "z1%d" % piece), Q)
+            features(piece * Q, Q, (q00, q01)[h] + (c0,), z1 + (0,), ("scalar", "scalar" if piece < 2 else "vector"))

@@ -1,6 +1,7 @@
 from contextlib import ExitStack
 
 import concourse.mybir as mybir
+from concourse.masks import make_identity
 
 F32 = mybir.dt.float32
 BF16 = mybir.dt.bfloat16
@@ -48,29 +49,46 @@ def tile_list_burrow_activity_features_kernel(
         pages = [keep.tile([P, S], F32, name="page%d" % i) for i in range(PAGES)]
         warm = keep.tile([P, 3], F32, name="warm")
 
+        wgs_t = keep.tile([P, PB], F32, name="wgs_t")
+        ident = keep.tile([P, P], F32, name="ident")
         nc.gpsimd.memset(t2s[:].bitcast(I32), 0)
-        nc.vector.memset(w2s[:].bitcast(I32), 0)
-        nc.gpsimd.memset(ts[:, : T // 2].bitcast(I32), 0)
-        nc.vector.memset(ts[:, T // 2 :].bitcast(I32), 0)
         nc.vector.memset(warm[:, 0:1], 1.0)
+        nc.vector.memset(w2s[:].bitcast(I32), 0)
+        nc.vector.memset(ts[:].bitcast(I32), 0)
+        make_identity(nc, ident[:])
 
         nc.sync.dma_start(offs2_t[:], offs2)
+        nc.sync.dma_start(wgs_t[:], wgs)
         nc.sync.dma_start(w2w[:].bitcast(I32), w2_words[0].bitcast(I32))
         nc.sync.dma_start(t2w[:], tab2_words[0].rearrange("p n t -> p (n t)").bitcast(I32))
         for q in range(4):
-            nc.scalar.dma_start(t2s[32 * q : 32 * q + 4, :].bitcast(I32), tab2_scales[0, 4 * q : 4 * q + 4, :].bitcast(I32))
+            nc.sync.dma_start(t2s[32 * q : 32 * q + 4, :].bitcast(I32), tab2_scales[0, 4 * q : 4 * q + 4, :].bitcast(I32))
         nc.scalar.activation(warm[:, 1:2], warm[:, 0:1], ACT.Ln)
         for q in range(4):
             nc.sync.dma_start(w2s[32 * q : 32 * q + 4, :].bitcast(I32), w2_scales[0, 4 * q : 4 * q + 4, :].bitcast(I32))
         for q in range(4):
-            nc.sync.dma_start(ts[32 * q : 32 * q + 8, :].bitcast(I32), tab_scales[:, 4 * q : 4 * q + 4, :].bitcast(I32))
+            nc.gpsimd.dma_start(ts[32 * q : 32 * q + 8, :].bitcast(I32), tab_scales[:, 4 * q : 4 * q + 4, :].bitcast(I32))
         nc.sync.dma_start(offs_t[:], offs)
         nc.sync.dma_start(pos_t[:], pos1)
-        wgs_rows = wgs.rearrange("(q t) m -> q (t m)", t=PACK)
-        for q in range(4):
-            nc.sync.dma_start(wg[32 * q : 32 * q + 32, :], wgs_rows)
         for page in pages:
-            nc.gpsimd.memset(page[:], 0.0)
+            nc.vector.memset(page[:], 0.0)
+        nc.gpsimd.dma_start(gain_t[:], gain.rearrange("(g p t) -> p g t", g=2, t=PACK))
+        with nc.allow_non_contiguous_dma(reason="one bias value a partition"):
+            nc.gpsimd.dma_start(base_t[:], base.rearrange("(c p) -> p c", p=P))
+
+        turned = psum.tile([P, PB // P, P], F32, name="acc")
+        for mb in range(PB // P):
+            nc.tensor.transpose(turned[:, mb, :], wgs_t[:, mb * P : (mb + 1) * P], ident[:])
+        for t in range(PACK):
+            dealt = rawp.tile([P, PB // P, 4, 32], F32, name="lev", bufs=8)
+            nc.scalar.copy(
+                dealt[:],
+                turned[:].rearrange("m b (q t) -> m b t q", t=PACK)[:, :, t, :].unsqueeze(2).broadcast_to([P, PB // P, 4, 32]),
+            )
+            back = psum.tile([P, PB // P, P], F32, name="acc")
+            for mb in range(PB // P):
+                nc.tensor.transpose(back[:, mb, :], dealt[:, mb, :, :].rearrange("m r q -> m (r q)"), ident[:])
+            nc.scalar.copy(wg[:, t * PB : (t + 1) * PB], back[:].rearrange("p b m -> p (b m)"))
 
         def load_w1(g, a):
             raw = rawp.tile([P, PACK, KP], F32, name="raw")
@@ -89,9 +107,6 @@ def tile_list_burrow_activity_features_kernel(
             nc.sync.dma_start(tw[a][:], tab_words[a].rearrange("p n t -> p (n t)").bitcast(I32))
         for a in range(2):
             w1raw[1, a] = load_w1(1, a)
-        nc.sync.dma_start(gain_t[:], gain.rearrange("(g p t) -> p g t", g=2, t=PACK))
-        with nc.allow_non_contiguous_dma(reason="one bias value a partition"):
-            nc.sync.dma_start(base_t[:], base.rearrange("(c p) -> p c", p=P))
 
         w2d = [keep.tile([P, 2 * KP], U8, name="w2d%d" % g, align_bytes=64) for g in range(2)]
         w2sd = [keep.tile([P, KP], U8, name="w2sd%d" % g, align_bytes=64) for g in range(2)]

@@ -14,14 +14,24 @@ FP4X4 = mybir.dt.float4_e2m1fn_x4
 ACT = mybir.ActivationFunctionType
 ALU = mybir.AluOpType
 
-K, K2, H, N, T, T3, S, PB = 1024, 512, 1024, 512, 4096, 2048, 1024, 512
-FLOPS = 2 * (K * H * S + K2 * H * PB + H * N * S)
+K, K2, H, N = 1024, 512, 1024, 512
+T, T2 = 4096, 2048
+S, M = 1024, 512
+FLOPS = 2 * (K * H * S + K2 * H * M + H * N * S)
 
 P = 128
 PACK = 4
-KP = P * PACK
+PASS = P * PACK
+QUADS = 4
+LIST_ROWS = 16
+GROUPS = H // PASS
+SLICES = GROUPS * PACK
 HALF = 512
-PAGES = 3
+PIECE = 256
+EARLY = 5
+GAIN_ON_VECTOR_FROM = 6
+SHARED_PIECES_FROM = 2
+STREAM_BUFS = 8
 
 
 def tile_list_burrow_activity_features_kernel(
@@ -30,267 +40,252 @@ def tile_list_burrow_activity_features_kernel(
     nc = tc.nc
     with ExitStack() as ctx:
         keep = ctx.enter_context(tc.tile_pool(name="keep", bufs=1))
-        rawp = ctx.enter_context(tc.tile_pool(name="rawp", bufs=4))
+        ring = ctx.enter_context(tc.tile_pool(name="ring", bufs=4))
         psum = ctx.enter_context(tc.psum_pool(name="psum", bufs=8))
 
-        offs_t = keep.tile([P, S // 16], U16, name="offs_t")
-        offs2_t = keep.tile([P, PB // 16], U16, name="offs2_t")
-        pos_t = keep.tile([P, PB // 16], U16, name="pos_t")
-        t2w = keep.tile([P, T3], I32, name="t2w")
-        t2s = keep.tile([P, T3], U8, name="t2s")
-        w2w = keep.tile([P, 2 * H], U8, name="w2w")
-        w2s = keep.tile([P, H], U8, name="w2s")
-        tw = [keep.tile([P, T], I32, name="tw%d" % a, align_bytes=64) for a in range(2)]
-        ts = keep.tile([P, T], U8, name="ts", align_bytes=64)
-        wg = keep.tile([P, PACK * PB], F32, name="wg")
-        gain_t = keep.tile([P, 2, PACK], F32, name="gain_t")
-        base_t = keep.tile([P, N // P], F32, name="base_t")
-        nbase = keep.tile([P, N // P], F32, name="nbase")
-        pages = [keep.tile([P, S], F32, name="page%d" % i) for i in range(PAGES)]
-        warm = keep.tile([P, 3], F32, name="warm")
-
-        wgs_t = keep.tile([P, PB], F32, name="wgs_t")
+        offs_t = keep.tile([P, S // LIST_ROWS], U16, name="offs_t")
+        offs2_t = keep.tile([P, M // LIST_ROWS], U16, name="offs2_t")
+        pos_t = keep.tile([P, M // LIST_ROWS], U16, name="pos_t")
+        tab2_w = keep.tile([P, T2], I32, name="tab2_w", align_bytes=64)
+        tab2_s = keep.tile([P, T2], U8, name="tab2_s", align_bytes=64)
+        w2_w = keep.tile([P, 2 * H], U8, name="w2_w")
+        w2_s = keep.tile([P, H], U8, name="w2_s", align_bytes=64)
+        tab_s = keep.tile([P, T], U8, name="tab_s", align_bytes=64)
+        wgs_dealt = keep.tile([P, PACK * M], F32, name="wgs_dealt")
+        gain_t = keep.tile([P, GROUPS, PACK], F32, name="gain_t")
+        minus_base = keep.tile([P, N // P], F32, name="minus_base")
+        wgs_t = keep.tile([P, M], F32, name="wgs_t", align_bytes=64)
         ident = keep.tile([P, P], F32, name="ident")
-        nc.gpsimd.memset(t2s[:].bitcast(I32), 0)
-        nc.vector.memset(warm[:, 0:1], 1.0)
-        nc.vector.memset(w2s[:].bitcast(I32), 0)
-        nc.vector.memset(ts[:].bitcast(I32), 0)
+
+        pages = []
+
+        def new_page(tag):
+            page = keep.tile([P, S], F32, name="page%d" % len(pages), tag=tag, align_bytes=64)
+            nc.gpsimd.memset(page[:], 0.0)
+            pages.append(page)
+
+        def load_scale_rows(tile, rows_of_quad, rows):
+            for quad in range(QUADS):
+                nc.sync.dma_start(tile[32 * quad : 32 * quad + rows, :].bitcast(I32), rows_of_quad(quad).bitcast(I32))
+
         make_identity(nc, ident[:])
+        nc.vector.memset(tab2_s[:].bitcast(I32), 0)
+        nc.vector.memset(w2_s[:].bitcast(I32), 0)
+        nc.vector.memset(tab_s[:].bitcast(I32), 0)
 
         nc.sync.dma_start(offs2_t[:], offs2)
         nc.sync.dma_start(wgs_t[:], wgs)
-        nc.sync.dma_start(w2w[:].bitcast(I32), w2_words[0].bitcast(I32))
-        nc.sync.dma_start(t2w[:], tab2_words[0].rearrange("p n t -> p (n t)").bitcast(I32))
-        for q in range(4):
-            nc.sync.dma_start(t2s[32 * q : 32 * q + 4, :].bitcast(I32), tab2_scales[0, 4 * q : 4 * q + 4, :].bitcast(I32))
-        nc.scalar.activation(warm[:, 1:2], warm[:, 0:1], ACT.Ln)
-        for q in range(4):
-            nc.sync.dma_start(w2s[32 * q : 32 * q + 4, :].bitcast(I32), w2_scales[0, 4 * q : 4 * q + 4, :].bitcast(I32))
-        for q in range(4):
-            nc.gpsimd.dma_start(ts[32 * q : 32 * q + 8, :].bitcast(I32), tab_scales[:, 4 * q : 4 * q + 4, :].bitcast(I32))
+        nc.sync.dma_start(w2_w[:].bitcast(I32), w2_words[0].bitcast(I32))
+        nc.sync.dma_start(tab2_w[:], tab2_words[0].rearrange("p n t -> p (n t)").bitcast(I32))
+        load_scale_rows(tab2_s, lambda quad: tab2_scales[0, 4 * quad : 4 * quad + 4, :], 4)
+        load_scale_rows(w2_s, lambda quad: w2_scales[0, 4 * quad : 4 * quad + 4, :], 4)
         nc.sync.dma_start(offs_t[:], offs)
+        load_scale_rows(tab_s, lambda quad: tab_scales[:, 4 * quad : 4 * quad + 4, :], 8)
         nc.sync.dma_start(pos_t[:], pos1)
-        for page in pages:
-            nc.vector.memset(page[:], 0.0)
-        nc.gpsimd.dma_start(gain_t[:], gain.rearrange("(g p t) -> p g t", g=2, t=PACK))
-        with nc.allow_non_contiguous_dma(reason="one bias value a partition"):
-            nc.gpsimd.dma_start(base_t[:], base.rearrange("(c p) -> p c", p=P))
+        new_page("page0")
 
-        turned = psum.tile([P, PB // P, P], F32, name="acc")
-        for mb in range(PB // P):
-            nc.tensor.transpose(turned[:, mb, :], wgs_t[:, mb * P : (mb + 1) * P], ident[:])
+        turned = psum.tile([P, M // P, P], F32, name="bank")
+        for blk in range(M // P):
+            nc.tensor.transpose(turned[:, blk, :], wgs_t[:, blk * P : (blk + 1) * P], ident[:])
         for t in range(PACK):
-            dealt = rawp.tile([P, PB // P, 4, 32], F32, name="lev", bufs=8)
-            nc.scalar.copy(
-                dealt[:],
-                turned[:].rearrange("m b (q t) -> m b t q", t=PACK)[:, :, t, :].unsqueeze(2).broadcast_to([P, PB // P, 4, 32]),
-            )
-            back = psum.tile([P, PB // P, P], F32, name="acc")
-            for mb in range(PB // P):
-                nc.tensor.transpose(back[:, mb, :], dealt[:, mb, :, :].rearrange("m r q -> m (r q)"), ident[:])
-            nc.scalar.copy(wg[:, t * PB : (t + 1) * PB], back[:].rearrange("p b m -> p (b m)"))
+            spread = ring.tile([P, M // P, QUADS, 32], F32, name="stream", bufs=STREAM_BUFS)
+            rows_t = turned[:].rearrange("m b (q t) -> m b t q", t=PACK)[:, :, t, :]
+            nc.scalar.copy(spread[:], rows_t.unsqueeze(2).broadcast_to([P, M // P, QUADS, 32]))
+            back = psum.tile([P, M // P, P], F32, name="bank")
+            for blk in range(M // P):
+                nc.tensor.transpose(back[:, blk, :], spread[:, blk, :, :].rearrange("m r q -> m (r q)"), ident[:])
+            nc.scalar.copy(wgs_dealt[:, t * M : (t + 1) * M], back[:].rearrange("p b m -> p (b m)"))
 
-        def load_w1(g, a):
-            raw = rawp.tile([P, PACK, KP], F32, name="raw")
-            nc.sync.dma_start(raw[:], w1[a * KP : (a + 1) * KP, g * KP : (g + 1) * KP].rearrange("(p j) c -> p j c", j=PACK))
+        def load_rows(raw, rows):
+            nc.sync.dma_start(raw[:], rows.rearrange("(p j) c -> p j c", j=PACK))
             return raw
 
-        def load_w4(g):
-            raw = rawp.tile([P, PACK, N], F32, name="raw")
-            nc.sync.dma_start(raw[:], w4[g * KP : (g + 1) * KP, :].rearrange("(p j) c -> p j c", j=PACK))
-            return raw
+        tab_w = {}
 
-        w1raw = {}
-        for a in range(2):
-            w1raw[0, a] = load_w1(0, a)
-        for a in range(2):
-            nc.sync.dma_start(tw[a][:], tab_words[a].rearrange("p n t -> p (n t)").bitcast(I32))
-        for a in range(2):
-            w1raw[1, a] = load_w1(1, a)
+        def load_table(a, tag):
+            tab_w[a] = keep.tile([P, T], I32, name="tab_w%d" % a, tag=tag, align_bytes=64)
+            nc.sync.dma_start(tab_w[a][:], tab_words[a].rearrange("p n t -> p (n t)").bitcast(I32))
 
-        w2d = [keep.tile([P, 2 * KP], U8, name="w2d%d" % g, align_bytes=64) for g in range(2)]
-        w2sd = [keep.tile([P, KP], U8, name="w2sd%d" % g, align_bytes=64) for g in range(2)]
-        v2w = keep.tile([P, PB], U32, name="v2w", align_bytes=64)
-        v2s = keep.tile([P, PB], U8, name="v2s", align_bytes=64)
-        def deal_words(g):
+        w1_raw = {}
+        for g in range(GROUPS):
+            for a in range(K // PASS):
+                raw = ring.tile([P, PACK, PASS], F32, name="raw")
+                w1_raw[g, a] = load_rows(raw, w1[a * PASS : (a + 1) * PASS, g * PASS : (g + 1) * PASS])
+        load_table(0, "tab_w0")
+        nc.sync.dma_start(gain_t[:], gain.rearrange("(g p t) -> p g t", g=GROUPS, t=PACK))
+
+        w2_wd = [keep.tile([P, 2 * PASS], U8, name="w2_wd%d" % g, align_bytes=64) for g in range(GROUPS)]
+        w2_sd = [keep.tile([P, PASS], U8, name="w2_sd%d" % g, align_bytes=64) for g in range(GROUPS)]
+        v2_w = keep.tile([P, M], U32, name="v2_w", align_bytes=64)
+        v2_s = keep.tile([P, M], U8, name="v2_s", align_bytes=64)
+        nc.vector.tensor_copy(v2_w[:], tab2_w[:].bitcast(U32).indirect(offs2_t[:]))
+        nc.vector.tensor_copy(v2_s[:], tab2_s[:].indirect(offs2_t[:]))
+        for g in range(GROUPS):
             nc.vector.tensor_copy(
-                w2d[g][:].rearrange("p (t m b) -> p t m b", t=PACK, b=2),
-                w2w[:, g * 2 * KP : (g + 1) * 2 * KP].rearrange("p (m t b) -> p t m b", t=PACK, b=2),
+                w2_wd[g][:].rearrange("p (t c e) -> p t c e", t=PACK, e=2),
+                w2_w[:, g * 2 * PASS : (g + 1) * 2 * PASS].rearrange("p (c t e) -> p t c e", t=PACK, e=2),
             )
-
-        def deal_scales(g):
             nc.vector.tensor_copy(
-                w2sd[g][:].rearrange("p (t m) -> p t m", t=PACK),
-                w2s[:, g * KP : (g + 1) * KP].rearrange("p (m t) -> p t m", t=PACK),
+                w2_sd[g][:].rearrange("p (t c) -> p t c", t=PACK),
+                w2_s[:, g * PASS : (g + 1) * PASS].rearrange("p (c t) -> p t c", t=PACK),
             )
-
-        nc.vector.tensor_copy(v2w[:], t2w[:].bitcast(U32).indirect(offs2_t[:]))
-        nc.vector.tensor_copy(v2s[:], t2s[:].indirect(offs2_t[:]))
-        for g in range(2):
-            deal_words(g)
-            deal_scales(g)
+        new_page("w2_s")
 
         b = []
-        for i in range(8):
+        for i in range(SLICES):
             g, t = divmod(i, PACK)
-            acc = psum.tile([P, PB], F32, name="acc")
+            acc = psum.tile([P, M], F32, name="bank")
             nc.tensor.matmul_mx(
                 out=acc[:],
-                lhsT=w2d[g][:, 2 * P * t : 2 * P * (t + 1)].bitcast(FP4X4),
-                lhsT_scale=w2sd[g][:, P * t : P * (t + 1)],
-                rhs=v2w[:].bitcast(FP8X4),
-                rhs_scale=v2s[:],
+                lhsT=w2_wd[g][:, 2 * P * t : 2 * P * (t + 1)].bitcast(FP4X4),
+                lhsT_scale=w2_sd[g][:, P * t : P * (t + 1)],
+                rhs=v2_w[:].bitcast(FP8X4),
+                rhs_scale=v2_s[:],
                 start=True,
                 stop=True,
             )
-            bi = keep.tile([P, PB], F32, name="b%d" % i, align_bytes=64)
-            nc.scalar.activation(bi[:], acc[:], ACT.Abs)
-            nc.scalar.activation(bi[:], bi[:], ACT.Ln, bias=1.0)
-            b.append(bi)
-
-        def page_of(i):
-            return pages[i if i < PAGES else 2 - min(i, 6) % 2]
+            b_i = keep.tile([P, M], F32, name="b%d" % i, align_bytes=64)
+            nc.scalar.activation(b_i[:], acc[:], ACT.Abs)
+            nc.scalar.activation(b_i[:], b_i[:], ACT.Ln, bias=1.0)
+            b.append(b_i)
 
         def scatter(i):
             t = i % PACK
-            nc.vector.tensor_tensor(page_of(i)[:].indirect(pos_t[:]), b[i][:], wg[:, t * PB : (t + 1) * PB], ALU.mult)
+            nc.vector.tensor_tensor(pages[i][:].indirect(pos_t[:]), b[i][:], wgs_dealt[:, t * M : (t + 1) * M], ALU.mult)
 
-        def quantise(name, grouped, width=KP, tag=None):
+        def quantise(name, grouped, width, tag=None):
             codes = keep.tile([P, width], U32, name=name + "_codes", tag=tag or name + "_codes", align_bytes=64)
             scales = keep.tile([P, width], U8, name=name + "_scales", align_bytes=64)
             nc.vector.quantize_mx(out=codes[:].bitcast(FP8X4), scales=scales[:], in_=grouped)
             return codes, scales
 
-        def cast_w1(g):
-            grouped = keep.tile([P, 2, PACK * KP], BF16, name="wbf%d" % g, align_bytes=64)
-            for a in range(2):
+        def round_w1(g):
+            grouped = keep.tile([P, K // PASS, PACK * PASS], BF16, name="w1_bf%d" % g, align_bytes=64)
+            for a in range(K // PASS):
                 nc.scalar.copy(
-                    grouped[:, a, :].rearrange("p (t m j) -> p m t j", t=PACK, j=PACK),
-                    w1raw[g, a][:].rearrange("p j (m t) -> p m t j", t=PACK),
+                    grouped[:, a, :].rearrange("p (t c j) -> p c t j", t=PACK, j=PACK),
+                    w1_raw[g, a][:].rearrange("p j (c t) -> p c t j", t=PACK),
                 )
             return grouped[:].rearrange("p a c -> p (a c)")
 
-        def cast_w4():
-            grouped = keep.tile([P, 2, PACK * N], BF16, name="w4bf", tag="tw1", align_bytes=64)
-            for g in range(2):
-                copy = nc.vector.tensor_copy if g == 1 else nc.scalar.copy
-                copy(grouped[:, g, :].rearrange("p (c j) -> p c j", j=PACK), w4raw[g][:].rearrange("p j c -> p c j"))
-            return grouped[:].rearrange("p g c -> p (g c)")
-
-        for i in range(PAGES):
+        for i in range(EARLY):
             scatter(i)
+            if i + 2 < EARLY:
+                new_page("b%d" % i)
+        base_t = keep.tile([P, N // P], F32, name="base_t", tag="b%d" % (EARLY - 1), align_bytes=64)
+        with nc.allow_non_contiguous_dma(reason="one bias value a partition"):
+            nc.gpsimd.dma_start(base_t[:], base.rearrange("(c p) -> p c", p=P))
 
-        cast0 = cast_w1(0)
-        nc.scalar.activation(warm[:, 2:3], b[7][:, 0:1], ACT.Sqrt, bias=1.0)
-        w4raw = [load_w4(g) for g in range(2)]
+        w1_bf = [round_w1(g) for g in range(GROUPS)]
+        w4_raw0 = keep.tile([P, PACK, N], F32, name="w4_raw0", tag="tab2_w", align_bytes=64)
+        load_rows(w4_raw0, w4[:PASS, :])
+        load_table(1, "tab2_s")
+        w4_raw1 = ring.tile([P, PACK, N], F32, name="raw")
+        load_rows(w4_raw1, w4[PASS:, :])
 
-        vw = {}
-        vs = {}
-        w1q = {}
+        v_w = {}
+        v_s = {}
+
+        def list_half(h):
+            return offs_t[:, h * HALF // LIST_ROWS : (h + 1) * HALF // LIST_ROWS]
 
         def gather_words(a, h, tag):
-            vw[a, h] = keep.tile([P, HALF], U32, name="vw%d%d" % (a, h), tag=tag, align_bytes=64)
-            nc.vector.tensor_copy(vw[a, h][:], tw[a][:].bitcast(U32).indirect(offs_t[:, h * HALF // 16 : (h + 1) * HALF // 16]))
+            v_w[a, h] = keep.tile([P, HALF], U32, name="v_w%d%d" % (a, h), tag=tag, align_bytes=64)
+            nc.vector.tensor_copy(v_w[a, h][:], tab_w[a][:].bitcast(U32).indirect(list_half(h)))
 
-        for h in range(2):
-            vs[h] = keep.tile([P, HALF], U8, name="vs%d" % h, align_bytes=64)
-            nc.vector.tensor_copy(vs[h][:], ts[:].indirect(offs_t[:, h * HALF // 16 : (h + 1) * HALF // 16]))
-        gather_words(0, 0, "vw00")
-        gather_words(0, 1, "vw01")
-        gather_words(1, 0, "vw10")
-        w1q[0] = quantise("w1q0", cast0, 2 * KP, tag="tw0")
-        gather_words(1, 1, "wbf0")
-        planes = {(g, h): keep.tile([P, PACK, HALF], BF16, name="zpl%d%d" % (g, h)) for g in range(2) for h in range(2)}
+        for h in range(S // HALF):
+            v_s[h] = keep.tile([P, HALF], U8, name="v_s%d" % h, align_bytes=64)
+            nc.vector.tensor_copy(v_s[h][:], tab_s[:].indirect(list_half(h)))
+        w1_q = [quantise("w1_q0", w1_bf[0], K, tag="b%d" % (EARLY - 2))]
+        gather_words(0, 0, "w1_bf0")
+        gather_words(0, 1, "v_w01")
 
-        def level(i, h):
+        w4_bf = keep.tile([P, GROUPS, PACK * N], BF16, name="w4_bf", tag="wgs_t", align_bytes=64)
+        for g, (copy, raw) in enumerate(((nc.scalar.copy, w4_raw0), (nc.vector.tensor_copy, w4_raw1))):
+            copy(w4_bf[:, g, :].rearrange("p (c j) -> p c j", j=PACK), raw[:].rearrange("p j c -> p c j"))
+
+        gather_words(1, 0, "v_w10")
+        gather_words(1, 1, "v_w11")
+
+        z_rows = {}
+        for g in range(GROUPS):
+            for h in range(S // HALF):
+                z_rows[g, h] = keep.tile([P, PACK, HALF], BF16, name="z_rows%d%d" % (g, h), align_bytes=64)
+
+        def make_z_rows(i):
             g, t = divmod(i, PACK)
-            acc = psum.tile([P, HALF], F32, name="acc")
-            for a in range(2):
-                codes, scales = w1q[g]
-                cols = slice(a * KP + P * t, a * KP + P * (t + 1))
-                nc.tensor.matmul_mx(
-                    out=acc[:],
-                    lhsT=codes[:, cols].bitcast(FP8X4),
-                    lhsT_scale=scales[:, cols],
-                    rhs=vw[a, h][:].bitcast(FP8X4),
-                    rhs_scale=vs[h][4 * a : P, :],
-                    start=(a == 0),
-                    stop=(a == 1),
-                )
-            if i == 6:
-                lev = keep.tile([P, HALF], F32, name="lev6%d" % h, tag="zpl0%d" % h)
-            else:
-                lev = rawp.tile([P, HALF], F32, name="lev", bufs=8)
-            dst = lev[:]
-            nc.vector.tensor_tensor(dst, acc[:], page_of(i)[:, h * HALF : (h + 1) * HALF], ALU.add)
-            nc.scalar.activation(dst, dst, ACT.Abs)
-            nc.scalar.activation(dst, dst, ACT.Sqrt, bias=1.0)
-            if i == 7:
-                nc.vector.tensor_scalar(planes[g, h][:, t, :], dst, gain_t[:, g, t : t + 1], None, ALU.mult)
-            else:
-                nc.scalar.activation(planes[g, h][:, t, :], dst, ACT.Copy, scale=gain_t[:, g, t : t + 1])
+            codes, scales = w1_q[g]
+            for h in range(S // HALF):
+                acc = psum.tile([P, HALF], F32, name="bank")
+                for a in range(K // PASS):
+                    cols = slice(a * PASS + P * t, a * PASS + P * (t + 1))
+                    nc.tensor.matmul_mx(
+                        out=acc[:],
+                        lhsT=codes[:, cols].bitcast(FP8X4),
+                        lhsT_scale=scales[:, cols],
+                        rhs=v_w[a, h][:].bitcast(FP8X4),
+                        rhs_scale=v_s[h][4 * a : P, :],
+                        start=(a == 0),
+                        stop=(a == K // PASS - 1),
+                    )
+                level = ring.tile([P, HALF], F32, name="stream", bufs=STREAM_BUFS)
+                nc.vector.tensor_tensor(level[:], acc[:], pages[i][:, h * HALF : (h + 1) * HALF], ALU.add)
+                nc.scalar.activation(level[:], level[:], ACT.Abs)
+                nc.scalar.activation(level[:], level[:], ACT.Sqrt, bias=1.0)
+                if i >= GAIN_ON_VECTOR_FROM:
+                    nc.vector.tensor_scalar(z_rows[g, h][:, t, :], level[:], gain_t[:, g, t : t + 1], None, ALU.mult)
+                else:
+                    nc.scalar.activation(z_rows[g, h][:, t, :], level[:], ACT.Copy, scale=gain_t[:, g, t : t + 1])
 
-        def z_on_vector(g, j0, width, tag):
+        def interleave_z(g, j0, width, tag):
             h, c0 = divmod(j0, HALF)
-            grouped = keep.tile([P, PACK * width], BF16, name="zbf%d_%d" % (g, j0), tag=tag, align_bytes=64)
+            grouped = keep.tile([P, PACK * width], BF16, name="z_bf%d_%d" % (g, j0), tag=tag, align_bytes=64)
             nc.vector.tensor_copy(
                 grouped[:].rearrange("p (c t) -> p c t", t=PACK),
-                planes[g, h][:, :, c0 : c0 + width].rearrange("p t c -> p c t"),
+                z_rows[g, h][:, :, c0 : c0 + width].rearrange("p t c -> p c t"),
             )
             return grouped[:]
 
-        def features(j0, width, z0, z1, engines):
+        nc.gpsimd.tensor_scalar(minus_base[:], base_t[:], -1.0, 0.0, ALU.mult, ALU.add)
+
+        for first in range(0, SLICES, 2):
+            make_z_rows(first)
+            make_z_rows(first + 1)
+            if first + 2 == PACK:
+                w1_q.append(quantise("w1_q1", w1_bf[1], K, tag="b%d" % EARLY))
+            if len(pages) < SLICES:
+                pages.append(pages[first + 1])
+                scatter(len(pages) - 1)
+
+        z0_bf = [interleave_z(0, 0, HALF, "b%d" % (SLICES - 1)), interleave_z(0, HALF, HALF, "z_rows00")]
+        z0_q = [quantise("z0_q%d" % h, z0_bf[h], HALF) for h in range(S // HALF)]
+        w4_codes, w4_scales = quantise("w4_q", w4_bf[:].rearrange("p g c -> p (g c)"), GROUPS * N, tag="z_rows01")
+
+        for piece in range(S // PIECE):
+            j0 = piece * PIECE
+            h, c0 = divmod(j0, HALF)
+            z1_codes, z1_scales = quantise("z1_q%d" % piece, interleave_z(1, j0, PIECE, "z1_bf%d" % piece), PIECE)
+            z_codes = (z0_q[h][0][:, c0 : c0 + PIECE], z1_codes[:])
+            z_scales = (z0_q[h][1][:, c0 : c0 + PIECE], z1_scales[:])
             for pair in range(2):
-                res = rawp.tile([P, 2, width], F32, name="res", bufs=8)
+                result = ring.tile([P, 2, PIECE], F32, name="result", bufs=STREAM_BUFS)
                 for e in range(2):
-                    c = 2 * pair + e
-                    acc = psum.tile([P, width], F32, name="acc")
-                    for g, (codes, scales, c0) in enumerate((z0, z1)):
+                    blk = 2 * pair + e
+                    acc = psum.tile([P, PIECE], F32, name="bank")
+                    for g in range(GROUPS):
+                        cols = slice(g * N + P * blk, g * N + P * (blk + 1))
                         nc.tensor.matmul_mx(
                             out=acc[:],
-                            lhsT=w4q[0][:, g * N + P * c : g * N + P * (c + 1)].bitcast(FP8X4),
-                            lhsT_scale=w4q[1][:, g * N + P * c : g * N + P * (c + 1)],
-                            rhs=codes[:, c0 : c0 + width].bitcast(FP8X4),
-                            rhs_scale=scales[:, c0 : c0 + width],
+                            lhsT=w4_codes[:, cols].bitcast(FP8X4),
+                            lhsT_scale=w4_scales[:, cols],
+                            rhs=z_codes[g].bitcast(FP8X4),
+                            rhs_scale=z_scales[g],
                             start=(g == 0),
-                            stop=(g == 1),
+                            stop=(g == GROUPS - 1),
                         )
-                    if engines[pair] == "vector":
-                        nc.vector.tensor_scalar(res[:, e, :], acc[:], base_t[:, c : c + 1], None, ALU.subtract)
+                    if pair == 1 and piece >= SHARED_PIECES_FROM:
+                        nc.vector.tensor_scalar(result[:, e, :], acc[:], base_t[:, blk : blk + 1], None, ALU.subtract)
                     else:
-                        nc.scalar.activation(res[:, e, :], acc[:], ACT.Identity, bias=nbase[:, c : c + 1])
-                rows = out[2 * P * pair : 2 * P * (pair + 1), j0 : j0 + width].rearrange("(e p) j -> p e j", p=P)
-                nc.sync.dma_start(rows, res[:])
-
-        nc.gpsimd.tensor_scalar(nbase[:], base_t[:], -1.0, 0.0, ALU.mult, ALU.add)
-
-        def levels(i):
-            for h in range(2):
-                level(i, h)
-
-        cast1 = cast_w1(1)
-        levels(0)
-        levels(1)
-        scatter(3)
-        w1q[1] = quantise("w1q1", cast1, 2 * KP, tag="b3")
-        cast4 = cast_w4()
-        levels(2)
-        scatter(4)
-        levels(3)
-        scatter(5)
-        levels(4)
-        scatter(6)
-        levels(5)
-        z00 = z_on_vector(0, 0, HALF, "b0")
-        z01 = z_on_vector(0, HALF, HALF, "b4")
-        q00 = quantise("zq00", z00)
-        levels(6)
-        scatter(7)
-        levels(7)
-        Q = HALF // 2
-        w4q = quantise("w4q", cast4, 2 * N, tag="b7")
-        q01 = quantise("zq01", z01, tag="b6")
-        for piece in range(4):
-            h, c0 = divmod(piece * Q, HALF)
-            z1 = quantise("zq1%d" % piece, z_on_vector(1, piece * Q, Q, "z1%d" % piece), Q)
-            features(piece * Q, Q, (q00, q01)[h] + (c0,), z1 + (0,), ("scalar", "scalar" if piece < 2 else "vector"))
+                        nc.scalar.activation(result[:, e, :], acc[:], ACT.Identity, bias=minus_base[:, blk : blk + 1])
+                rows = out[2 * P * pair : 2 * P * (pair + 1), j0 : j0 + PIECE].rearrange("(e p) j -> p e j", p=P)
+                nc.sync.dma_start(rows, result[:])

from contextlib import ExitStack

import concourse.mybir as mybir
from concourse.masks import make_identity

F32 = mybir.dt.float32
BF16 = mybir.dt.bfloat16
I32 = mybir.dt.int32
U32 = mybir.dt.uint32
U16 = mybir.dt.uint16
U8 = mybir.dt.uint8
FP8X4 = mybir.dt.float8_e4m3fn_x4
FP4X4 = mybir.dt.float4_e2m1fn_x4
ACT = mybir.ActivationFunctionType
ALU = mybir.AluOpType

K, K2, H, N = 1024, 512, 1024, 512
T, T2 = 4096, 2048
S, M = 1024, 512
FLOPS = 2 * (K * H * S + K2 * H * M + H * N * S)

P = 128
PACK = 4
PASS = P * PACK
QUADS = 4
LIST_ROWS = 16
GROUPS = H // PASS
SLICES = GROUPS * PACK
HALF = 512
PIECE = 256
EARLY = 5
GAIN_ON_VECTOR_FROM = 6
SHARED_PIECES_FROM = 2
STREAM_BUFS = 8


def tile_list_burrow_activity_features_kernel(
    tc, tab_words, tab_scales, offs, tab2_words, tab2_scales, offs2, pos1, w1, w2_words, w2_scales, wgs, gain, w4, base, out
):
    nc = tc.nc
    with ExitStack() as ctx:
        keep = ctx.enter_context(tc.tile_pool(name="keep", bufs=1))
        ring = ctx.enter_context(tc.tile_pool(name="ring", bufs=4))
        psum = ctx.enter_context(tc.psum_pool(name="psum", bufs=8))

        offs_t = keep.tile([P, S // LIST_ROWS], U16, name="offs_t")
        offs2_t = keep.tile([P, M // LIST_ROWS], U16, name="offs2_t")
        pos_t = keep.tile([P, M // LIST_ROWS], U16, name="pos_t")
        tab2_w = keep.tile([P, T2], I32, name="tab2_w", align_bytes=64)
        tab2_s = keep.tile([P, T2], U8, name="tab2_s", align_bytes=64)
        w2_w = keep.tile([P, 2 * H], U8, name="w2_w")
        w2_s = keep.tile([P, H], U8, name="w2_s", align_bytes=64)
        tab_s = keep.tile([P, T], U8, name="tab_s", align_bytes=64)
        wgs_dealt = keep.tile([P, PACK * M], F32, name="wgs_dealt")
        gain_t = keep.tile([P, GROUPS, PACK], F32, name="gain_t")
        minus_base = keep.tile([P, N // P], F32, name="minus_base")
        wgs_t = keep.tile([P, M], F32, name="wgs_t", align_bytes=64)
        ident = keep.tile([P, P], F32, name="ident")

        pages = []

        def new_page(tag):
            page = keep.tile([P, S], F32, name="page%d" % len(pages), tag=tag, align_bytes=64)
            nc.gpsimd.memset(page[:], 0.0)
            pages.append(page)

        def load_scale_rows(tile, rows_of_quad, rows):
            for quad in range(QUADS):
                nc.sync.dma_start(tile[32 * quad : 32 * quad + rows, :].bitcast(I32), rows_of_quad(quad).bitcast(I32))

        make_identity(nc, ident[:])
        nc.vector.memset(tab2_s[:].bitcast(I32), 0)
        nc.vector.memset(w2_s[:].bitcast(I32), 0)
        nc.vector.memset(tab_s[:].bitcast(I32), 0)

        nc.sync.dma_start(offs2_t[:], offs2)
        nc.sync.dma_start(wgs_t[:], wgs)
        nc.sync.dma_start(w2_w[:].bitcast(I32), w2_words[0].bitcast(I32))
        nc.sync.dma_start(tab2_w[:], tab2_words[0].rearrange("p n t -> p (n t)").bitcast(I32))
        load_scale_rows(tab2_s, lambda quad: tab2_scales[0, 4 * quad : 4 * quad + 4, :], 4)
        load_scale_rows(w2_s, lambda quad: w2_scales[0, 4 * quad : 4 * quad + 4, :], 4)
        nc.sync.dma_start(offs_t[:], offs)
        load_scale_rows(tab_s, lambda quad: tab_scales[:, 4 * quad : 4 * quad + 4, :], 8)
        nc.sync.dma_start(pos_t[:], pos1)
        new_page("page0")

        turned = psum.tile([P, M // P, P], F32, name="bank")
        for blk in range(M // P):
            nc.tensor.transpose(turned[:, blk, :], wgs_t[:, blk * P : (blk + 1) * P], ident[:])
        for t in range(PACK):
            spread = ring.tile([P, M // P, QUADS, 32], F32, name="stream", bufs=STREAM_BUFS)
            rows_t = turned[:].rearrange("m b (q t) -> m b t q", t=PACK)[:, :, t, :]
            nc.scalar.copy(spread[:], rows_t.unsqueeze(2).broadcast_to([P, M // P, QUADS, 32]))
            back = psum.tile([P, M // P, P], F32, name="bank")
            for blk in range(M // P):
                nc.tensor.transpose(back[:, blk, :], spread[:, blk, :, :].rearrange("m r q -> m (r q)"), ident[:])
            nc.scalar.copy(wgs_dealt[:, t * M : (t + 1) * M], back[:].rearrange("p b m -> p (b m)"))

        def load_rows(raw, rows):
            nc.sync.dma_start(raw[:], rows.rearrange("(p j) c -> p j c", j=PACK))
            return raw

        tab_w = {}

        def load_table(a, tag):
            tab_w[a] = keep.tile([P, T], I32, name="tab_w%d" % a, tag=tag, align_bytes=64)
            nc.sync.dma_start(tab_w[a][:], tab_words[a].rearrange("p n t -> p (n t)").bitcast(I32))

        w1_raw = {}
        for g in range(GROUPS):
            for a in range(K // PASS):
                raw = ring.tile([P, PACK, PASS], F32, name="raw")
                w1_raw[g, a] = load_rows(raw, w1[a * PASS : (a + 1) * PASS, g * PASS : (g + 1) * PASS])
        load_table(0, "tab_w0")
        nc.sync.dma_start(gain_t[:], gain.rearrange("(g p t) -> p g t", g=GROUPS, t=PACK))

        w2_wd = [keep.tile([P, 2 * PASS], U8, name="w2_wd%d" % g, align_bytes=64) for g in range(GROUPS)]
        w2_sd = [keep.tile([P, PASS], U8, name="w2_sd%d" % g, align_bytes=64) for g in range(GROUPS)]
        v2_w = keep.tile([P, M], U32, name="v2_w", align_bytes=64)
        v2_s = keep.tile([P, M], U8, name="v2_s", align_bytes=64)
        nc.vector.tensor_copy(v2_w[:], tab2_w[:].bitcast(U32).indirect(offs2_t[:]))
        nc.vector.tensor_copy(v2_s[:], tab2_s[:].indirect(offs2_t[:]))
        for g in range(GROUPS):
            nc.vector.tensor_copy(
                w2_wd[g][:].rearrange("p (t c e) -> p t c e", t=PACK, e=2),
                w2_w[:, g * 2 * PASS : (g + 1) * 2 * PASS].rearrange("p (c t e) -> p t c e", t=PACK, e=2),
            )
            nc.vector.tensor_copy(
                w2_sd[g][:].rearrange("p (t c) -> p t c", t=PACK),
                w2_s[:, g * PASS : (g + 1) * PASS].rearrange("p (c t) -> p t c", t=PACK),
            )
        new_page("w2_s")

        b = []
        for i in range(SLICES):
            g, t = divmod(i, PACK)
            acc = psum.tile([P, M], F32, name="bank")
            nc.tensor.matmul_mx(
                out=acc[:],
                lhsT=w2_wd[g][:, 2 * P * t : 2 * P * (t + 1)].bitcast(FP4X4),
                lhsT_scale=w2_sd[g][:, P * t : P * (t + 1)],
                rhs=v2_w[:].bitcast(FP8X4),
                rhs_scale=v2_s[:],
                start=True,
                stop=True,
            )
            b_i = keep.tile([P, M], F32, name="b%d" % i, align_bytes=64)
            nc.scalar.activation(b_i[:], acc[:], ACT.Abs)
            nc.scalar.activation(b_i[:], b_i[:], ACT.Ln, bias=1.0)
            b.append(b_i)

        def scatter(i):
            t = i % PACK
            nc.vector.tensor_tensor(pages[i][:].indirect(pos_t[:]), b[i][:], wgs_dealt[:, t * M : (t + 1) * M], ALU.mult)

        def quantise(name, grouped, width, tag=None):
            codes = keep.tile([P, width], U32, name=name + "_codes", tag=tag or name + "_codes", align_bytes=64)
            scales = keep.tile([P, width], U8, name=name + "_scales", align_bytes=64)
            nc.vector.quantize_mx(out=codes[:].bitcast(FP8X4), scales=scales[:], in_=grouped)
            return codes, scales

        def round_w1(g):
            grouped = keep.tile([P, K // PASS, PACK * PASS], BF16, name="w1_bf%d" % g, align_bytes=64)
            for a in range(K // PASS):
                nc.scalar.copy(
                    grouped[:, a, :].rearrange("p (t c j) -> p c t j", t=PACK, j=PACK),
                    w1_raw[g, a][:].rearrange("p j (c t) -> p c t j", t=PACK),
                )
            return grouped[:].rearrange("p a c -> p (a c)")

        for i in range(EARLY):
            scatter(i)
            if i + 2 < EARLY:
                new_page("b%d" % i)
        base_t = keep.tile([P, N // P], F32, name="base_t", tag="b%d" % (EARLY - 1), align_bytes=64)
        with nc.allow_non_contiguous_dma(reason="one bias value a partition"):
            nc.gpsimd.dma_start(base_t[:], base.rearrange("(c p) -> p c", p=P))

        w1_bf = [round_w1(g) for g in range(GROUPS)]
        w4_raw0 = keep.tile([P, PACK, N], F32, name="w4_raw0", tag="tab2_w", align_bytes=64)
        load_rows(w4_raw0, w4[:PASS, :])
        load_table(1, "tab2_s")
        w4_raw1 = ring.tile([P, PACK, N], F32, name="raw")
        load_rows(w4_raw1, w4[PASS:, :])

        v_w = {}
        v_s = {}

        def list_half(h):
            return offs_t[:, h * HALF // LIST_ROWS : (h + 1) * HALF // LIST_ROWS]

        def gather_words(a, h, tag):
            v_w[a, h] = keep.tile([P, HALF], U32, name="v_w%d%d" % (a, h), tag=tag, align_bytes=64)
            nc.vector.tensor_copy(v_w[a, h][:], tab_w[a][:].bitcast(U32).indirect(list_half(h)))

        for h in range(S // HALF):
            v_s[h] = keep.tile([P, HALF], U8, name="v_s%d" % h, align_bytes=64)
            nc.vector.tensor_copy(v_s[h][:], tab_s[:].indirect(list_half(h)))
        w1_q = [quantise("w1_q0", w1_bf[0], K, tag="b%d" % (EARLY - 2))]
        gather_words(0, 0, "w1_bf0")
        gather_words(0, 1, "v_w01")

        w4_bf = keep.tile([P, GROUPS, PACK * N], BF16, name="w4_bf", tag="wgs_t", align_bytes=64)
        for g, (copy, raw) in enumerate(((nc.scalar.copy, w4_raw0), (nc.vector.tensor_copy, w4_raw1))):
            copy(w4_bf[:, g, :].rearrange("p (c j) -> p c j", j=PACK), raw[:].rearrange("p j c -> p c j"))

        gather_words(1, 0, "v_w10")
        gather_words(1, 1, "v_w11")

        z_rows = {}
        for g in range(GROUPS):
            for h in range(S // HALF):
                z_rows[g, h] = keep.tile([P, PACK, HALF], BF16, name="z_rows%d%d" % (g, h), align_bytes=64)

        def make_z_rows(i):
            g, t = divmod(i, PACK)
            codes, scales = w1_q[g]
            for h in range(S // HALF):
                acc = psum.tile([P, HALF], F32, name="bank")
                for a in range(K // PASS):
                    cols = slice(a * PASS + P * t, a * PASS + P * (t + 1))
                    nc.tensor.matmul_mx(
                        out=acc[:],
                        lhsT=codes[:, cols].bitcast(FP8X4),
                        lhsT_scale=scales[:, cols],
                        rhs=v_w[a, h][:].bitcast(FP8X4),
                        rhs_scale=v_s[h][4 * a : P, :],
                        start=(a == 0),
                        stop=(a == K // PASS - 1),
                    )
                level = ring.tile([P, HALF], F32, name="stream", bufs=STREAM_BUFS)
                nc.vector.tensor_tensor(level[:], acc[:], pages[i][:, h * HALF : (h + 1) * HALF], ALU.add)
                nc.scalar.activation(level[:], level[:], ACT.Abs)
                nc.scalar.activation(level[:], level[:], ACT.Sqrt, bias=1.0)
                if i >= GAIN_ON_VECTOR_FROM:
                    nc.vector.tensor_scalar(z_rows[g, h][:, t, :], level[:], gain_t[:, g, t : t + 1], None, ALU.mult)
                else:
                    nc.scalar.activation(z_rows[g, h][:, t, :], level[:], ACT.Copy, scale=gain_t[:, g, t : t + 1])

        def interleave_z(g, j0, width, tag):
            h, c0 = divmod(j0, HALF)
            grouped = keep.tile([P, PACK * width], BF16, name="z_bf%d_%d" % (g, j0), tag=tag, align_bytes=64)
            nc.vector.tensor_copy(
                grouped[:].rearrange("p (c t) -> p c t", t=PACK),
                z_rows[g, h][:, :, c0 : c0 + width].rearrange("p t c -> p c t"),
            )
            return grouped[:]

        nc.gpsimd.tensor_scalar(minus_base[:], base_t[:], -1.0, 0.0, ALU.mult, ALU.add)

        for first in range(0, SLICES, 2):
            make_z_rows(first)
            make_z_rows(first + 1)
            if first + 2 == PACK:
                w1_q.append(quantise("w1_q1", w1_bf[1], K, tag="b%d" % EARLY))
            if len(pages) < SLICES:
                pages.append(pages[first + 1])
                scatter(len(pages) - 1)

        z0_bf = [interleave_z(0, 0, HALF, "b%d" % (SLICES - 1)), interleave_z(0, HALF, HALF, "z_rows00")]
        z0_q = [quantise("z0_q%d" % h, z0_bf[h], HALF) for h in range(S // HALF)]
        w4_codes, w4_scales = quantise("w4_q", w4_bf[:].rearrange("p g c -> p (g c)"), GROUPS * N, tag="z_rows01")

        for piece in range(S // PIECE):
            j0 = piece * PIECE
            h, c0 = divmod(j0, HALF)
            z1_codes, z1_scales = quantise("z1_q%d" % piece, interleave_z(1, j0, PIECE, "z1_bf%d" % piece), PIECE)
            z_codes = (z0_q[h][0][:, c0 : c0 + PIECE], z1_codes[:])
            z_scales = (z0_q[h][1][:, c0 : c0 + PIECE], z1_scales[:])
            for pair in range(2):
                result = ring.tile([P, 2, PIECE], F32, name="result", bufs=STREAM_BUFS)
                for e in range(2):
                    blk = 2 * pair + e
                    acc = psum.tile([P, PIECE], F32, name="bank")
                    for g in range(GROUPS):
                        cols = slice(g * N + P * blk, g * N + P * (blk + 1))
                        nc.tensor.matmul_mx(
                            out=acc[:],
                            lhsT=w4_codes[:, cols].bitcast(FP8X4),
                            lhsT_scale=w4_scales[:, cols],
                            rhs=z_codes[g].bitcast(FP8X4),
                            rhs_scale=z_scales[g],
                            start=(g == 0),
                            stop=(g == GROUPS - 1),
                        )
                    if pair == 1 and piece >= SHARED_PIECES_FROM:
                        nc.vector.tensor_scalar(result[:, e, :], acc[:], base_t[:, blk : blk + 1], None, ALU.subtract)
                    else:
                        nc.scalar.activation(result[:, e, :], acc[:], ACT.Identity, bias=minus_base[:, blk : blk + 1])
                rows = out[2 * P * pair : 2 * P * (pair + 1), j0 : j0 + PIECE].rearrange("(e p) j -> p e j", p=P)
                nc.sync.dma_start(rows, result[:])
